import numpy as np
import ml_dtypes


def mxq(x, axis, fmt="e4m3"):
    dtype, down = {"e4m3": (ml_dtypes.float8_e4m3fn, 7), "e5m2": (ml_dtypes.float8_e5m2, 14)}[fmt]
    v = np.moveaxis(np.asarray(x, np.float32).astype(ml_dtypes.bfloat16).astype(np.float64), axis, -1)
    blocks = v.reshape(v.shape[:-1] + (-1, 32))
    amax = np.abs(blocks).max(-1, keepdims=True)
    byte = np.maximum(np.where(amax > 0, np.frexp(amax)[1] - 1 + 127, 0) - down, 1)
    scale = np.exp2(byte - 127.0)
    codes = (blocks / scale).astype(np.float32).astype(dtype).astype(np.float64)
    return np.moveaxis((codes * scale).reshape(v.shape), -1, axis)


WIDE = False


def mx_kscale(k):
    if not WIDE:
        return np.ones(k)
    levels = np.array([10, -10, 5, -5, 0])
    if k % 512:
        return np.exp2(np.random.permutation(np.resize(levels, k // 32))).repeat(32)
    a = np.empty((k // 512, 16))
    for p in range(k // 512):
        a[p, :8] = np.random.permutation(np.resize(levels, 8))
        for g in range(8):
            far = levels[np.abs(levels - a[p, g]) >= 10]
            a[p, g + 8] = far[np.random.randint(len(far))]
    return np.exp2(a.ravel()).repeat(32)


def f64(x):
    return np.asarray(x).astype(np.float64)


def striped(idx):
    return np.tile(idx.reshape(-1, 16).T, (8, 1)).astype(np.uint16)


def unstriped(offs):
    return offs[:16].T.reshape(-1).astype(np.int64)


def pack_weight(w):
    k, n = w.shape
    w = f64(np.asarray(w, np.float32).astype(ml_dtypes.bfloat16)).reshape(k // 32, 32, n)
    amax = np.abs(w).max(1)
    byte = np.clip(np.where(amax > 0, np.frexp(amax)[1] - 1 + 127 - 7, 1), 1, 254)
    scaled = (w * np.exp2(127.0 - byte)[:, None, :]).reshape(k, n).astype(np.float32)
    words = np.ascontiguousarray(scaled.reshape(k // 512, 128, 4, n).transpose(0, 1, 3, 2)).astype(ml_dtypes.float8_e4m3fn).view(np.uint8)
    return words, np.ascontiguousarray(byte.astype(np.uint8).reshape(k // 512, 16, n))


def unpack_weight(words, scales):
    g, p, n, _ = words.shape
    vals = np.ascontiguousarray(words).view(ml_dtypes.float8_e4m3fn).astype(np.float64) * np.repeat(np.exp2(scales.astype(np.float64) - 127.0), 8, axis=1)[..., None]
    return vals.transpose(0, 1, 3, 2).reshape(g * 512, n)


def relu(v):
    return np.maximum(v, 0.0)


K, T, S, H, N, V = 512, 1024, 512, 512, 128, 256
P = 2 ** 7


def setup_inputs():
    n = np.random.standard_normal
    s = mx_kscale(K)[:, None]
    u = mx_kscale(H)
    packed_xT = pack_weight(n((K, T)) * s)
    return {
        "x_words": packed_xT[0],
        "x_scales": packed_xT[1],
        "w1": (n((K, H)) / np.sqrt(K) / s * u).astype(np.float32),
        "w2": (n((H, N)) / np.sqrt(H) / u[:, None]).astype(np.float32),
        "w3": (n((K, N)) / np.sqrt(K) / s).astype(np.float32),
        "score": (np.tile(np.random.uniform(0.2, 1.0, S), (P, 1))).astype(np.float32),
        "offs": striped(np.random.permutation(T)[:S]),
        "kept": striped(np.random.permutation(S)[:V]),
    }


def reference(x_words, x_scales, w1, w2, w3, score, offs, kept):
    xq = unpack_weight(x_words, x_scales)[:, unstriped(offs)]
    h = relu(mxq(f64(w1), 0, "e4m3").T @ xq)
    z = h[:, unstriped(kept)] * (f64(score)[:1][:, unstriped(kept)])
    rr = relu(mxq(f64(w2), 0, "e4m3").T @ mxq(z, 0, "e4m3"))
    up = np.zeros((N, S))
    up[:, unstriped(kept)] = rr
    y = mxq(f64(w3), 0, "e4m3").T @ xq
    return up + y

@@ -1,0 +1,134 @@
+from contextlib import ExitStack
+
+import concourse.mybir as mybir
+
+K, T, S, H, N, V = 512, 1024, 512, 512, 128, 256
+FLOPS = 2 * K * H * S + 2 * H * N * V + 2 * K * N * S
+
+F32 = mybir.dt.float32
+BF16 = mybir.dt.bfloat16
+I32 = mybir.dt.int32
+U32 = mybir.dt.uint32
+U16 = mybir.dt.uint16
+U8 = mybir.dt.uint8
+FP8X4 = mybir.dt.float8_e4m3fn_x4
+RELU = mybir.ActivationFunctionType.Relu
+COPY = mybir.ActivationFunctionType.Copy
+MULT = mybir.AluOpType.mult
+ADD = mybir.AluOpType.add
+
+P = 128
+PACK = 4
+
+
+def tile_picked_ygunet_relu_p_kernel(tc, x_words, x_scales, w1, w2, w3, score, offs, kept, out):
+    nc = tc.nc
+    with ExitStack() as ctx:
+        sb = ctx.enter_context(tc.tile_pool(name="sb", bufs=1))
+        ps = ctx.enter_context(tc.psum_pool(name="ps", bufs=1))
+
+        offs_sb = sb.tile([P, S // 16], U16, name="offs_sb")
+        kept_sb = sb.tile([P, V // 16], U16, name="kept_sb")
+        words_all = sb.tile([P, T], I32, name="words_all")
+        scales_all = sb.tile([P, T], U8, name="scales_all")
+        up = sb.tile([P, S], F32, name="up")
+
+        nc.vector.memset(scales_all[:].bitcast(I32), 0)
+        nc.sync.dma_start(words_all[:], x_words[0].rearrange("p c r -> p (c r)").bitcast(I32))
+        nc.sync.dma_start(offs_sb[:], offs)
+        for q in range(4):
+            nc.scalar.dma_start(scales_all[32 * q : 32 * q + 4, :].bitcast(I32), x_scales[0, 4 * q : 4 * q + 4, :].bitcast(I32))
+        w1_rows = w1.rearrange("(p j) c -> p j c", j=PACK)
+        w1_raw = []
+        for half in range(2):
+            raw = sb.tile([P, PACK, H // 2], F32, name=f"w1_raw{half}")
+            nc.sync.dma_start(raw[:], w1_rows[:, :, half * (H // 2) : (half + 1) * (H // 2)])
+            w1_raw.append(raw)
+        nc.sync.dma_start(kept_sb[:], kept)
+        w2_raw = sb.tile([P, PACK, N], F32, name="w2_raw")
+        nc.sync.dma_start(w2_raw[:], w2.rearrange("(p j) c -> p j c", j=PACK))
+        score_sb = sb.tile([P, S], F32, name="score_sb")
+        nc.sync.dma_start(score_sb[:], score)
+        w3_raw = sb.tile([P, PACK, N], F32, name="w3_raw")
+        nc.sync.dma_start(w3_raw[:], w3.rearrange("(p j) c -> p j c", j=PACK))
+        nc.vector.memset(up[:], 0.0)
+
+        x_codes = sb.tile([P, S], U32, name="x_codes", align_bytes=64)
+        x_plane = sb.tile([P, S], U8, name="x_plane", align_bytes=64)
+        nc.vector.tensor_copy(x_codes[:], words_all[:].bitcast(U32).indirect(offs_sb[:]))
+        nc.vector.tensor_copy(x_plane[:], scales_all[:].indirect(offs_sb[:]))
+
+        w1_bf = sb.tile([P, PACK, P * PACK], BF16, name="w1_bf", align_bytes=64)
+        w1_dst = w1_bf[:].rearrange("p t (m j) -> p m t j", j=PACK)
+        nc.scalar.activation(w1_dst[:, 0:64], w1_raw[0][:].rearrange("p j (m t) -> p m t j", t=PACK), COPY)
+        nc.vector.tensor_copy(w1_dst[:, 64:128], w1_raw[1][:].rearrange("p j (m t) -> p m t j", t=PACK))
+
+        def quantize(name, grouped, width):
+            codes = sb.tile([P, width], U32, name=name + "_codes", align_bytes=64)
+            plane = sb.tile([P, width], U8, name=name + "_plane", align_bytes=64)
+            nc.vector.quantize_mx(out=codes[:].bitcast(FP8X4), scales=plane[:], in_=grouped)
+            return codes, plane
+
+        def product(acc, lhs, rhs):
+            nc.tensor.matmul_mx(out=acc, lhsT=lhs[0][:].bitcast(FP8X4), lhsT_scale=lhs[1][:],
+                                rhs=rhs[0][:].bitcast(FP8X4), rhs_scale=rhs[1][:], start=True, stop=True)
+
+        def interleave_views(dst, src):
+            return (dst.rearrange("p (c i t) -> p c t i", i=4, t=PACK), src.rearrange("p t (c i) -> p c t i", i=4))
+
+        h = []
+        for t in range(PACK):
+            w1_q = quantize(f"w1_{t}", w1_bf[:, t, :], P)
+            acc = ps.tile([P, S], F32, name=f"h_acc{t}")
+            product(acc[:], w1_q, (x_codes, x_plane))
+            h_t = sb.tile([P, S], F32, name=f"h{t}")
+            nc.scalar.activation(h_t[:], acc[:], RELU)
+            h.append(h_t)
+            if t == 0:
+                w2_bf = sb.tile([P, N * PACK], BF16, name="w2_bf", align_bytes=64)
+                d, s = interleave_views(w2_bf[:], w2_raw[:])
+                nc.scalar.activation(d, s, COPY)
+
+        score_kept = sb.tile([P, V], F32, name="score_kept")
+        nc.vector.tensor_copy(score_kept[:], score_sb[:].indirect(kept_sb[:]))
+        w2_q = quantize("w2", w2_bf[:], N)
+
+        z = sb.tile([P, PACK, V], F32, name="z")
+        for t in range(PACK - 1):
+            nc.vector.tensor_tensor(z[:, t, :], h[t][:].indirect(kept_sb[:]), score_kept[:], MULT)
+        part = V // 2
+        for a in range(2):
+            nc.vector.tensor_tensor(z[:, 3, a * part : (a + 1) * part], h[3][:].indirect(kept_sb[:, a * 8 : (a + 1) * 8]),
+                                    score_kept[:, a * part : (a + 1) * part], MULT)
+        z_bf = []
+        for a in range(2):
+            zb = sb.tile([P, part * PACK], BF16, name=f"z_bf{a}", align_bytes=64)
+            d, s = interleave_views(zb[:], z[:, :, a * part : (a + 1) * part])
+            if a == 0:
+                nc.vector.tensor_copy(d, s)
+            else:
+                nc.scalar.activation(d, s, COPY)
+            z_bf.append(zb)
+
+        w3_bf = sb.tile([P, N * PACK], BF16, name="w3_bf", align_bytes=64)
+        rr = []
+        for a in range(2):
+            z_q = quantize(f"z{a}", z_bf[a][:], part)
+            acc = ps.tile([P, part], F32, name=f"rr_acc{a}")
+            product(acc[:], w2_q, z_q)
+            rr_a = sb.tile([P, part], F32, name=f"rr{a}")
+            nc.scalar.activation(rr_a[:], acc[:], RELU)
+            rr.append(rr_a)
+        d, s = interleave_views(w3_bf[:], w3_raw[:])
+        nc.scalar.activation(d, s, COPY)
+        nc.vector.tensor_copy(up[:].indirect(kept_sb[:, 0:8]), rr[0][:])
+        w3_q = quantize("w3", w3_bf[:], N)
+        y_acc = ps.tile([P, S], F32, name="y_acc")
+        product(y_acc[:], w3_q, (x_codes, x_plane))
+        nc.vector.tensor_copy(up[:].indirect(kept_sb[:, 8:16]), rr[1][:])
+
+        for c in range(2):
+            cols = slice(c * (S // 2), (c + 1) * (S // 2))
+            res = sb.tile([P, S // 2], F32, name=f"res{c}")
+            nc.vector.tensor_tensor(res[:], y_acc[:, cols], up[:, cols], ADD)
+            nc.sync.dma_start(out[:, cols], res[:])

@@ -34,64 +34,73 @@ def tile_picked_ygunet_relu_p_kernel(tc, x_words, x_scales, w1, w2, w3, score, o
         up = sb.tile([P, S], F32, name="up")
 
         nc.vector.memset(scales_all[:].bitcast(I32), 0)
-        nc.sync.dma_start(words_all[:], x_words[0].rearrange("p c r -> p (c r)").bitcast(I32))
-        nc.sync.dma_start(offs_sb[:], offs)
-        for q in range(4):
-            nc.scalar.dma_start(scales_all[32 * q : 32 * q + 4, :].bitcast(I32), x_scales[0, 4 * q : 4 * q + 4, :].bitcast(I32))
         w1_rows = w1.rearrange("(p j) c -> p j c", j=PACK)
         w1_raw = []
         for half in range(2):
             raw = sb.tile([P, PACK, H // 2], F32, name=f"w1_raw{half}")
             nc.sync.dma_start(raw[:], w1_rows[:, :, half * (H // 2) : (half + 1) * (H // 2)])
             w1_raw.append(raw)
+            if half == 0:
+                nc.sync.dma_start(offs_sb[:], offs)
+                for q in range(4):
+                    nc.sync.dma_start(scales_all[32 * q : 32 * q + 4, :].bitcast(I32), x_scales[0, 4 * q : 4 * q + 4, :].bitcast(I32))
+                nc.sync.dma_start(words_all[:], x_words[0].rearrange("p c r -> p (c r)").bitcast(I32))
         nc.sync.dma_start(kept_sb[:], kept)
-        w2_raw = sb.tile([P, PACK, N], F32, name="w2_raw")
-        nc.sync.dma_start(w2_raw[:], w2.rearrange("(p j) c -> p j c", j=PACK))
         score_sb = sb.tile([P, S], F32, name="score_sb")
         nc.sync.dma_start(score_sb[:], score)
+        w2_raw = sb.tile([P, PACK, N], F32, name="w2_raw")
+        nc.sync.dma_start(w2_raw[:], w2.rearrange("(p j) c -> p j c", j=PACK))
         w3_raw = sb.tile([P, PACK, N], F32, name="w3_raw")
         nc.sync.dma_start(w3_raw[:], w3.rearrange("(p j) c -> p j c", j=PACK))
         nc.vector.memset(up[:], 0.0)
 
         x_codes = sb.tile([P, S], U32, name="x_codes", align_bytes=64)
         x_plane = sb.tile([P, S], U8, name="x_plane", align_bytes=64)
-        nc.vector.tensor_copy(x_codes[:], words_all[:].bitcast(U32).indirect(offs_sb[:]))
         nc.vector.tensor_copy(x_plane[:], scales_all[:].indirect(offs_sb[:]))
+        nc.vector.tensor_copy(x_codes[:], words_all[:].bitcast(U32).indirect(offs_sb[:]))
 
-        w1_bf = sb.tile([P, PACK, P * PACK], BF16, name="w1_bf", align_bytes=64)
-        w1_dst = w1_bf[:].rearrange("p t (m j) -> p m t j", j=PACK)
-        nc.scalar.activation(w1_dst[:, 0:64], w1_raw[0][:].rearrange("p j (m t) -> p m t j", t=PACK), COPY)
-        nc.vector.tensor_copy(w1_dst[:, 64:128], w1_raw[1][:].rearrange("p j (m t) -> p m t j", t=PACK))
+        w1_bf = [sb.tile([P, 2, P * PACK], BF16, name=f"w1_bf{u}", align_bytes=64) for u in range(2)]
+        w1_dst = [bf[:].rearrange("p t (m j) -> p m t j", j=PACK) for bf in w1_bf]
+        w1_src = [raw[:].rearrange("p j (m t) -> p m t j", t=PACK) for raw in w1_raw]
+        for u in range(2):
+            nc.scalar.activation(w1_dst[u][:, 0:64], w1_src[0][:, :, 2 * u : 2 * u + 2], COPY)
+        nc.vector.tensor_copy(w1_dst[0][:, 64:128], w1_src[1][:, :, 0:2])
+        nc.scalar.activation(w1_dst[1][:, 64:128], w1_src[1][:, :, 2:4], COPY)
 
         def quantize(name, grouped, width):
-            codes = sb.tile([P, width], U32, name=name + "_codes", align_bytes=64)
-            plane = sb.tile([P, width], U8, name=name + "_plane", align_bytes=64)
+            codes = sb.tile([P, width], U32, name=name + "_codes", tag=name + "_codes", align_bytes=64)
+            plane = sb.tile([P, width], U8, name=name + "_plane", tag=name + "_plane", align_bytes=64)
             nc.vector.quantize_mx(out=codes[:].bitcast(FP8X4), scales=plane[:], in_=grouped)
-            return codes, plane
+            return codes[:], plane[:]
 
         def product(acc, lhs, rhs):
-            nc.tensor.matmul_mx(out=acc, lhsT=lhs[0][:].bitcast(FP8X4), lhsT_scale=lhs[1][:],
-                                rhs=rhs[0][:].bitcast(FP8X4), rhs_scale=rhs[1][:], start=True, stop=True)
+            nc.tensor.matmul_mx(out=acc, lhsT=lhs[0].bitcast(FP8X4), lhsT_scale=lhs[1],
+                                rhs=rhs[0].bitcast(FP8X4), rhs_scale=rhs[1], start=True, stop=True)
 
         def interleave_views(dst, src):
             return (dst.rearrange("p (c i t) -> p c t i", i=4, t=PACK), src.rearrange("p t (c i) -> p c t i", i=4))
 
         h = []
         for t in range(PACK):
-            w1_q = quantize(f"w1_{t}", w1_bf[:, t, :], P)
-            acc = ps.tile([P, S], F32, name=f"h_acc{t}")
-            product(acc[:], w1_q, (x_codes, x_plane))
+            w1_q = quantize(f"w1_{t}", w1_bf[t // 2][:, t % 2, :], P)
             h_t = sb.tile([P, S], F32, name=f"h{t}")
-            nc.scalar.activation(h_t[:], acc[:], RELU)
+            pieces = 2
+            width = S // pieces
+            for c in range(pieces):
+                cols = slice(c * width, (c + 1) * width)
+                acc = ps.tile([P, width], F32, name=f"h_acc{t}_{c}", tag=f"bank{2 * t + c}")
+                product(acc[:], w1_q, (x_codes[:, cols], x_plane[:, cols]))
+                nc.scalar.activation(h_t[:, cols], acc[:], RELU)
             h.append(h_t)
-            if t == 0:
-                w2_bf = sb.tile([P, N * PACK], BF16, name="w2_bf", align_bytes=64)
-                d, s = interleave_views(w2_bf[:], w2_raw[:])
-                nc.scalar.activation(d, s, COPY)
 
         score_kept = sb.tile([P, V], F32, name="score_kept")
         nc.vector.tensor_copy(score_kept[:], score_sb[:].indirect(kept_sb[:]))
-        w2_q = quantize("w2", w2_bf[:], N)
+        w2_bf = sb.tile([P, N * PACK], BF16, name="w2_bf", tag="w1_3_codes", align_bytes=64)
+        d, s = interleave_views(w2_bf[:], w2_raw[:])
+        nc.scalar.activation(d, s, COPY)
+        w3_bf = sb.tile([P, N * PACK], BF16, name="w3_bf", tag="w1_3_plane", align_bytes=64)
+        d, s = interleave_views(w3_bf[:], w3_raw[:])
+        nc.scalar.activation(d, s, COPY)
 
         z = sb.tile([P, PACK, V], F32, name="z")
         for t in range(PACK - 1):
@@ -110,21 +119,19 @@ def tile_picked_ygunet_relu_p_kernel(tc, x_words, x_scales, w1, w2, w3, score, o
                 nc.scalar.activation(d, s, COPY)
             z_bf.append(zb)
 
-        w3_bf = sb.tile([P, N * PACK], BF16, name="w3_bf", align_bytes=64)
+        w2_q = quantize("w2", w2_bf[:], N)
         rr = []
         for a in range(2):
             z_q = quantize(f"z{a}", z_bf[a][:], part)
-            acc = ps.tile([P, part], F32, name=f"rr_acc{a}")
+            acc = ps.tile([P, part], F32, name=f"rr_acc{a}", tag=f"bank{a}")
             product(acc[:], w2_q, z_q)
             rr_a = sb.tile([P, part], F32, name=f"rr{a}")
             nc.scalar.activation(rr_a[:], acc[:], RELU)
             rr.append(rr_a)
-        d, s = interleave_views(w3_bf[:], w3_raw[:])
-        nc.scalar.activation(d, s, COPY)
-        nc.vector.tensor_copy(up[:].indirect(kept_sb[:, 0:8]), rr[0][:])
         w3_q = quantize("w3", w3_bf[:], N)
-        y_acc = ps.tile([P, S], F32, name="y_acc")
-        product(y_acc[:], w3_q, (x_codes, x_plane))
+        y_acc = ps.tile([P, S], F32, name="y_acc", tag="bank1")
+        product(y_acc[:], w3_q, (x_codes[:], x_plane[:]))
+        nc.vector.tensor_copy(up[:].indirect(kept_sb[:, 0:8]), rr[0][:])
         nc.vector.tensor_copy(up[:].indirect(kept_sb[:, 8:16]), rr[1][:])
 
         for c in range(2):

@@ -34,17 +34,16 @@ def tile_picked_ygunet_relu_p_kernel(tc, x_words, x_scales, w1, w2, w3, score, o
         up = sb.tile([P, S], F32, name="up")
 
         nc.vector.memset(scales_all[:].bitcast(I32), 0)
+        nc.sync.dma_start(words_all[:], x_words[0].rearrange("p c r -> p (c r)").bitcast(I32))
+        nc.sync.dma_start(offs_sb[:], offs)
+        for q in range(4):
+            nc.sync.dma_start(scales_all[32 * q : 32 * q + 4, :].bitcast(I32), x_scales[0, 4 * q : 4 * q + 4, :].bitcast(I32))
         w1_rows = w1.rearrange("(p j) c -> p j c", j=PACK)
         w1_raw = []
         for half in range(2):
-            raw = sb.tile([P, PACK, H // 2], F32, name=f"w1_raw{half}")
-            nc.sync.dma_start(raw[:], w1_rows[:, :, half * (H // 2) : (half + 1) * (H // 2)])
+            raw = sb.tile([P, 2, H], F32, name=f"w1_raw{half}")
+            nc.sync.dma_start(raw[:], w1_rows[:, 2 * half : 2 * half + 2, :])
             w1_raw.append(raw)
-            if half == 0:
-                nc.sync.dma_start(offs_sb[:], offs)
-                for q in range(4):
-                    nc.sync.dma_start(scales_all[32 * q : 32 * q + 4, :].bitcast(I32), x_scales[0, 4 * q : 4 * q + 4, :].bitcast(I32))
-                nc.sync.dma_start(words_all[:], x_words[0].rearrange("p c r -> p (c r)").bitcast(I32))
         nc.sync.dma_start(kept_sb[:], kept)
         score_sb = sb.tile([P, S], F32, name="score_sb")
         nc.sync.dma_start(score_sb[:], score)
@@ -56,16 +55,17 @@ def tile_picked_ygunet_relu_p_kernel(tc, x_words, x_scales, w1, w2, w3, score, o
 
         x_codes = sb.tile([P, S], U32, name="x_codes", align_bytes=64)
         x_plane = sb.tile([P, S], U8, name="x_plane", align_bytes=64)
-        nc.vector.tensor_copy(x_plane[:], scales_all[:].indirect(offs_sb[:]))
         nc.vector.tensor_copy(x_codes[:], words_all[:].bitcast(U32).indirect(offs_sb[:]))
+        nc.vector.tensor_copy(x_plane[:], scales_all[:].indirect(offs_sb[:]))
 
         w1_bf = [sb.tile([P, 2, P * PACK], BF16, name=f"w1_bf{u}", align_bytes=64) for u in range(2)]
         w1_dst = [bf[:].rearrange("p t (m j) -> p m t j", j=PACK) for bf in w1_bf]
         w1_src = [raw[:].rearrange("p j (m t) -> p m t j", t=PACK) for raw in w1_raw]
         for u in range(2):
-            nc.scalar.activation(w1_dst[u][:, 0:64], w1_src[0][:, :, 2 * u : 2 * u + 2], COPY)
-        nc.vector.tensor_copy(w1_dst[0][:, 64:128], w1_src[1][:, :, 0:2])
-        nc.scalar.activation(w1_dst[1][:, 64:128], w1_src[1][:, :, 2:4], COPY)
+            nc.scalar.activation(w1_dst[u][:, :, :, 0:2], w1_src[0][:, :, 2 * u : 2 * u + 2], COPY)
+        for t in range(2):
+            nc.vector.tensor_copy(w1_dst[0][:, :, t, 2:4], w1_src[1][:, :, t])
+        nc.scalar.activation(w1_dst[1][:, :, :, 2:4], w1_src[1][:, :, 2:4], COPY)
 
         def quantize(name, grouped, width):
             codes = sb.tile([P, width], U32, name=name + "_codes", tag=name + "_codes", align_bytes=64)

@@ -19,6 +19,13 @@ ADD = mybir.AluOpType.add
 
 P = 128
 PACK = 4
+QUADRANT = 32
+PER_COLUMN = 16
+HALF_S = S // 2
+HALF_V = V // 2
+PARTS = 4
+PART = V // PARTS
+VECTOR_PARTS = 2
 
 
 def tile_picked_ygunet_relu_p_kernel(tc, x_words, x_scales, w1, w2, w3, score, offs, kept, out):
@@ -27,17 +34,34 @@ def tile_picked_ygunet_relu_p_kernel(tc, x_words, x_scales, w1, w2, w3, score, o
         sb = ctx.enter_context(tc.tile_pool(name="sb", bufs=1))
         ps = ctx.enter_context(tc.psum_pool(name="ps", bufs=1))
 
-        offs_sb = sb.tile([P, S // 16], U16, name="offs_sb")
-        kept_sb = sb.tile([P, V // 16], U16, name="kept_sb")
+        def quantize(name, grouped, width):
+            codes = sb.tile([P, width], U32, name=name + "_codes", tag=name + "_codes", align_bytes=64)
+            scales = sb.tile([P, width], U8, name=name + "_plane", tag=name + "_plane", align_bytes=64)
+            nc.vector.quantize_mx(out=codes[:].bitcast(FP8X4), scales=scales[:], in_=grouped)
+            return codes[:], scales[:]
+
+        def product(acc, lhs, rhs):
+            nc.tensor.matmul_mx(out=acc, lhsT=lhs[0].bitcast(FP8X4), lhsT_scale=lhs[1],
+                                rhs=rhs[0].bitcast(FP8X4), rhs_scale=rhs[1], start=True, stop=True)
+
+        def interleave_views(dst, src):
+            return (dst.rearrange("p (c i j) -> p c j i", i=4, j=PACK), src.rearrange("p j (c i) -> p c j i", i=4))
+
+        def list_columns(lo, hi):
+            return kept_sb[:, lo // PER_COLUMN : hi // PER_COLUMN]
+
+        offs_sb = sb.tile([P, S // PER_COLUMN], U16, name="offs_sb")
+        kept_sb = sb.tile([P, V // PER_COLUMN], U16, name="kept_sb")
         words_all = sb.tile([P, T], I32, name="words_all")
         scales_all = sb.tile([P, T], U8, name="scales_all")
-        up = sb.tile([P, S], F32, name="up")
+        up = [sb.tile([P, S], F32, name=f"up{u}") for u in range(2)]
 
         nc.vector.memset(scales_all[:].bitcast(I32), 0)
         nc.sync.dma_start(words_all[:], x_words[0].rearrange("p c r -> p (c r)").bitcast(I32))
         nc.sync.dma_start(offs_sb[:], offs)
-        for q in range(4):
-            nc.sync.dma_start(scales_all[32 * q : 32 * q + 4, :].bitcast(I32), x_scales[0, 4 * q : 4 * q + 4, :].bitcast(I32))
+        for q in range(P // QUADRANT):
+            nc.sync.dma_start(scales_all[QUADRANT * q : QUADRANT * q + 4, :].bitcast(I32),
+                              x_scales[0, 4 * q : 4 * q + 4, :].bitcast(I32))
         w1_rows = w1.rearrange("(p j) c -> p j c", j=PACK)
         w1_raw = []
         for half in range(2):
@@ -51,7 +75,8 @@ def tile_picked_ygunet_relu_p_kernel(tc, x_words, x_scales, w1, w2, w3, score, o
         nc.sync.dma_start(w2_raw[:], w2.rearrange("(p j) c -> p j c", j=PACK))
         w3_raw = sb.tile([P, PACK, N], F32, name="w3_raw")
         nc.sync.dma_start(w3_raw[:], w3.rearrange("(p j) c -> p j c", j=PACK))
-        nc.vector.memset(up[:], 0.0)
+        for window in up:
+            nc.vector.memset(window[:], 0.0)
 
         x_codes = sb.tile([P, S], U32, name="x_codes", align_bytes=64)
         x_plane = sb.tile([P, S], U8, name="x_plane", align_bytes=64)
@@ -67,75 +92,67 @@ def tile_picked_ygunet_relu_p_kernel(tc, x_words, x_scales, w1, w2, w3, score, o
             nc.vector.tensor_copy(w1_dst[0][:, :, t, 2:4], w1_src[1][:, :, t])
         nc.scalar.activation(w1_dst[1][:, :, :, 2:4], w1_src[1][:, :, 2:4], COPY)
 
-        def quantize(name, grouped, width):
-            codes = sb.tile([P, width], U32, name=name + "_codes", tag=name + "_codes", align_bytes=64)
-            plane = sb.tile([P, width], U8, name=name + "_plane", tag=name + "_plane", align_bytes=64)
-            nc.vector.quantize_mx(out=codes[:].bitcast(FP8X4), scales=plane[:], in_=grouped)
-            return codes[:], plane[:]
-
-        def product(acc, lhs, rhs):
-            nc.tensor.matmul_mx(out=acc, lhsT=lhs[0].bitcast(FP8X4), lhsT_scale=lhs[1],
-                                rhs=rhs[0].bitcast(FP8X4), rhs_scale=rhs[1], start=True, stop=True)
-
-        def interleave_views(dst, src):
-            return (dst.rearrange("p (c i t) -> p c t i", i=4, t=PACK), src.rearrange("p t (c i) -> p c t i", i=4))
-
         h = []
         for t in range(PACK):
             w1_q = quantize(f"w1_{t}", w1_bf[t // 2][:, t % 2, :], P)
             h_t = sb.tile([P, S], F32, name=f"h{t}")
-            pieces = 2
-            width = S // pieces
-            for c in range(pieces):
-                cols = slice(c * width, (c + 1) * width)
-                acc = ps.tile([P, width], F32, name=f"h_acc{t}_{c}", tag=f"bank{2 * t + c}")
+            for c in range(2):
+                cols = slice(c * HALF_S, (c + 1) * HALF_S)
+                acc = ps.tile([P, HALF_S], F32, name=f"h_acc{t}_{c}", tag=f"bank{2 * t + c}")
                 product(acc[:], w1_q, (x_codes[:, cols], x_plane[:, cols]))
                 nc.scalar.activation(h_t[:, cols], acc[:], RELU)
             h.append(h_t)
 
         score_kept = sb.tile([P, V], F32, name="score_kept")
         nc.vector.tensor_copy(score_kept[:], score_sb[:].indirect(kept_sb[:]))
+
         w2_bf = sb.tile([P, N * PACK], BF16, name="w2_bf", tag="w1_3_codes", align_bytes=64)
-        d, s = interleave_views(w2_bf[:], w2_raw[:])
-        nc.scalar.activation(d, s, COPY)
+        nc.scalar.activation(*interleave_views(w2_bf[:], w2_raw[:]), COPY)
         w3_bf = sb.tile([P, N * PACK], BF16, name="w3_bf", tag="w1_3_plane", align_bytes=64)
-        d, s = interleave_views(w3_bf[:], w3_raw[:])
-        nc.scalar.activation(d, s, COPY)
+        nc.scalar.activation(*interleave_views(w3_bf[:], w3_raw[:]), COPY)
 
         z = sb.tile([P, PACK, V], F32, name="z")
-        for t in range(PACK - 1):
+        last = PACK - 1
+        for t in range(last):
             nc.vector.tensor_tensor(z[:, t, :], h[t][:].indirect(kept_sb[:]), score_kept[:], MULT)
-        part = V // 2
-        for a in range(2):
-            nc.vector.tensor_tensor(z[:, 3, a * part : (a + 1) * part], h[3][:].indirect(kept_sb[:, a * 8 : (a + 1) * 8]),
-                                    score_kept[:, a * part : (a + 1) * part], MULT)
+        for lo in range(0, V, HALF_V):
+            nc.vector.tensor_tensor(z[:, last, lo : lo + HALF_V], h[last][:].indirect(list_columns(lo, lo + HALF_V)),
+                                    score_kept[:, lo : lo + HALF_V], MULT)
+
         z_bf = []
-        for a in range(2):
-            zb = sb.tile([P, part * PACK], BF16, name=f"z_bf{a}", align_bytes=64)
-            d, s = interleave_views(zb[:], z[:, :, a * part : (a + 1) * part])
-            if a == 0:
-                nc.vector.tensor_copy(d, s)
+        for a in range(PARTS):
+            zb = sb.tile([P, PART * PACK], BF16, name=f"z_bf{a}", align_bytes=64)
+            dst, src = interleave_views(zb[:], z[:, :, a * PART : (a + 1) * PART])
+            if a < VECTOR_PARTS:
+                nc.vector.tensor_copy(dst, src)
             else:
-                nc.scalar.activation(d, s, COPY)
+                nc.scalar.activation(dst, src, COPY)
             z_bf.append(zb)
 
         w2_q = quantize("w2", w2_bf[:], N)
         rr = []
-        for a in range(2):
-            z_q = quantize(f"z{a}", z_bf[a][:], part)
-            acc = ps.tile([P, part], F32, name=f"rr_acc{a}", tag=f"bank{a}")
+        for a in range(PARTS):
+            z_q = quantize(f"z{a}", z_bf[a][:], PART)
+            acc = ps.tile([P, PART], F32, name=f"rr_acc{a}", tag=f"bank{a}")
             product(acc[:], w2_q, z_q)
-            rr_a = sb.tile([P, part], F32, name=f"rr{a}")
+            rr_a = sb.tile([P, PART], F32, name=f"rr{a}")
             nc.scalar.activation(rr_a[:], acc[:], RELU)
             rr.append(rr_a)
-        w3_q = quantize("w3", w3_bf[:], N)
-        y_acc = ps.tile([P, S], F32, name="y_acc", tag="bank1")
-        product(y_acc[:], w3_q, (x_codes[:], x_plane[:]))
-        nc.vector.tensor_copy(up[:].indirect(kept_sb[:, 0:8]), rr[0][:])
-        nc.vector.tensor_copy(up[:].indirect(kept_sb[:, 8:16]), rr[1][:])
 
-        for c in range(2):
-            cols = slice(c * (S // 2), (c + 1) * (S // 2))
-            res = sb.tile([P, S // 2], F32, name=f"res{c}")
-            nc.vector.tensor_tensor(res[:], y_acc[:, cols], up[:, cols], ADD)
+        w3_q = quantize("w3", w3_bf[:], N)
+        y_acc = ps.tile([P, S], F32, name="y_acc", tag=f"bank{PARTS - 2}")
+        product(y_acc[:], w3_q, (x_codes[:], x_plane[:]))
+
+        for a in range(PARTS):
+            nc.vector.tensor_copy(up[a % 2][:].indirect(list_columns(a * PART, (a + 1) * PART)), rr[a][:])
+
+        halves = [slice(c * HALF_S, (c + 1) * HALF_S) for c in range(2)]
+        partial = []
+        for c, cols in enumerate(halves):
+            y_plus = sb.tile([P, HALF_S], F32, name=f"partial{c}")
+            nc.vector.tensor_tensor(y_plus[:], y_acc[:, cols], up[0][:, cols], ADD)
+            partial.append(y_plus)
+        for c, cols in enumerate(halves):
+            res = sb.tile([P, HALF_S], F32, name=f"res{c}")
+            nc.vector.tensor_tensor(res[:], partial[c][:], up[1][:, cols], ADD)
             nc.sync.dma_start(out[:, cols], res[:])

@@ -54,7 +54,7 @@ def tile_picked_ygunet_relu_p_kernel(tc, x_words, x_scales, w1, w2, w3, score, o
         kept_sb = sb.tile([P, V // PER_COLUMN], U16, name="kept_sb")
         words_all = sb.tile([P, T], I32, name="words_all")
         scales_all = sb.tile([P, T], U8, name="scales_all")
-        up = [sb.tile([P, S], F32, name=f"up{u}") for u in range(2)]
+        up = sb.tile([P, S], F32, name="up")
 
         nc.vector.memset(scales_all[:].bitcast(I32), 0)
         nc.sync.dma_start(words_all[:], x_words[0].rearrange("p c r -> p (c r)").bitcast(I32))
@@ -75,15 +75,14 @@ def tile_picked_ygunet_relu_p_kernel(tc, x_words, x_scales, w1, w2, w3, score, o
         nc.sync.dma_start(w2_raw[:], w2.rearrange("(p j) c -> p j c", j=PACK))
         w3_raw = sb.tile([P, PACK, N], F32, name="w3_raw")
         nc.sync.dma_start(w3_raw[:], w3.rearrange("(p j) c -> p j c", j=PACK))
-        for window in up:
-            nc.vector.memset(window[:], 0.0)
+        nc.vector.memset(up[:], 0.0)
 
         x_codes = sb.tile([P, S], U32, name="x_codes", align_bytes=64)
         x_plane = sb.tile([P, S], U8, name="x_plane", align_bytes=64)
         nc.vector.tensor_copy(x_codes[:], words_all[:].bitcast(U32).indirect(offs_sb[:]))
         nc.vector.tensor_copy(x_plane[:], scales_all[:].indirect(offs_sb[:]))
 
-        w1_bf = [sb.tile([P, 2, P * PACK], BF16, name=f"w1_bf{u}", align_bytes=64) for u in range(2)]
+        w1_bf = [sb.tile([P, 2, P * PACK], BF16, name=f"w1_bf{u}", tag=f"w1_bf{u}", align_bytes=64) for u in range(2)]
         w1_dst = [bf[:].rearrange("p t (m j) -> p m t j", j=PACK) for bf in w1_bf]
         w1_src = [raw[:].rearrange("p j (m t) -> p m t j", t=PACK) for raw in w1_raw]
         for u in range(2):
@@ -93,12 +92,15 @@ def tile_picked_ygunet_relu_p_kernel(tc, x_words, x_scales, w1, w2, w3, score, o
         nc.scalar.activation(w1_dst[1][:, :, :, 2:4], w1_src[1][:, :, 2:4], COPY)
 
         h = []
+        pieces = 0
         for t in range(PACK):
             w1_q = quantize(f"w1_{t}", w1_bf[t // 2][:, t % 2, :], P)
             h_t = sb.tile([P, S], F32, name=f"h{t}")
-            for c in range(2):
-                cols = slice(c * HALF_S, (c + 1) * HALF_S)
-                acc = ps.tile([P, HALF_S], F32, name=f"h_acc{t}_{c}", tag=f"bank{2 * t + c}")
+            width = HALF_S // 2 if t == 0 else HALF_S
+            for lo in range(0, S, width):
+                cols = slice(lo, lo + width)
+                acc = ps.tile([P, width], F32, name=f"h_acc{t}_{lo}", tag=f"bank{pieces % 8}")
+                pieces = pieces + 1
                 product(acc[:], w1_q, (x_codes[:, cols], x_plane[:, cols]))
                 nc.scalar.activation(h_t[:, cols], acc[:], RELU)
             h.append(h_t)
@@ -106,8 +108,10 @@ def tile_picked_ygunet_relu_p_kernel(tc, x_words, x_scales, w1, w2, w3, score, o
         score_kept = sb.tile([P, V], F32, name="score_kept")
         nc.vector.tensor_copy(score_kept[:], score_sb[:].indirect(kept_sb[:]))
 
-        w2_bf = sb.tile([P, N * PACK], BF16, name="w2_bf", tag="w1_3_codes", align_bytes=64)
-        nc.scalar.activation(*interleave_views(w2_bf[:], w2_raw[:]), COPY)
+        w2_bf = sb.tile([P, N * PACK], BF16, name="w2_bf", tag="w1_bf1", align_bytes=64)
+        nc.vector.tensor_copy(*interleave_views(w2_bf[:], w2_raw[:]))
+        w2_q = quantize("w2", w2_bf[:], N)
+
         w3_bf = sb.tile([P, N * PACK], BF16, name="w3_bf", tag="w1_3_plane", align_bytes=64)
         nc.scalar.activation(*interleave_views(w3_bf[:], w3_raw[:]), COPY)
 
@@ -115,44 +119,31 @@ def tile_picked_ygunet_relu_p_kernel(tc, x_words, x_scales, w1, w2, w3, score, o
         last = PACK - 1
         for t in range(last):
             nc.vector.tensor_tensor(z[:, t, :], h[t][:].indirect(kept_sb[:]), score_kept[:], MULT)
-        for lo in range(0, V, HALF_V):
-            nc.vector.tensor_tensor(z[:, last, lo : lo + HALF_V], h[last][:].indirect(list_columns(lo, lo + HALF_V)),
-                                    score_kept[:, lo : lo + HALF_V], MULT)
+        for lo, hi in ((0, PART), (PART, 2 * PART), (2 * PART, V)):
+            nc.vector.tensor_tensor(z[:, last, lo:hi], h[last][:].indirect(list_columns(lo, hi)), score_kept[:, lo:hi], MULT)
 
-        z_bf = []
+        rr = sb.tile([P, V], F32, name="rr")
         for a in range(PARTS):
-            zb = sb.tile([P, PART * PACK], BF16, name=f"z_bf{a}", align_bytes=64)
+            zb = sb.tile([P, PART * PACK], BF16, name=f"z_bf{a}", tag=f"z_bf{a % 3}", align_bytes=64)
             dst, src = interleave_views(zb[:], z[:, :, a * PART : (a + 1) * PART])
-            if a < VECTOR_PARTS:
+            if a in (3,):
                 nc.vector.tensor_copy(dst, src)
             else:
                 nc.scalar.activation(dst, src, COPY)
-            z_bf.append(zb)
-
-        w2_q = quantize("w2", w2_bf[:], N)
-        rr = []
-        for a in range(PARTS):
-            z_q = quantize(f"z{a}", z_bf[a][:], PART)
-            acc = ps.tile([P, PART], F32, name=f"rr_acc{a}", tag=f"bank{a}")
+            z_q = quantize(f"z{a}", zb[:], PART)
+            acc = ps.tile([P, PART], F32, name=f"rr_acc{a}", tag=f"bank{a + 2}")
             product(acc[:], w2_q, z_q)
-            rr_a = sb.tile([P, PART], F32, name=f"rr{a}")
-            nc.scalar.activation(rr_a[:], acc[:], RELU)
-            rr.append(rr_a)
+            nc.scalar.activation(rr[:, a * PART : (a + 1) * PART], acc[:], RELU)
 
         w3_q = quantize("w3", w3_bf[:], N)
-        y_acc = ps.tile([P, S], F32, name="y_acc", tag=f"bank{PARTS - 2}")
+        y_acc = ps.tile([P, S], F32, name="y_acc", tag="bank4")
         product(y_acc[:], w3_q, (x_codes[:], x_plane[:]))
 
-        for a in range(PARTS):
-            nc.vector.tensor_copy(up[a % 2][:].indirect(list_columns(a * PART, (a + 1) * PART)), rr[a][:])
+        for lo, hi in ((0, PART), (PART, V)):
+            nc.vector.tensor_copy(up[:].indirect(list_columns(lo, hi)), rr[:, lo:hi])
 
-        halves = [slice(c * HALF_S, (c + 1) * HALF_S) for c in range(2)]
-        partial = []
-        for c, cols in enumerate(halves):
-            y_plus = sb.tile([P, HALF_S], F32, name=f"partial{c}")
-            nc.vector.tensor_tensor(y_plus[:], y_acc[:, cols], up[0][:, cols], ADD)
-            partial.append(y_plus)
-        for c, cols in enumerate(halves):
+        for c in range(2):
+            cols = slice(c * HALF_S, (c + 1) * HALF_S)
             res = sb.tile([P, HALF_S], F32, name=f"res{c}")
-            nc.vector.tensor_tensor(res[:], partial[c][:], up[1][:, cols], ADD)
+            nc.vector.tensor_tensor(res[:], y_acc[:, cols], up[:, cols], ADD)
             nc.sync.dma_start(out[:, cols], res[:])

@@ -71,10 +71,10 @@ def tile_picked_ygunet_relu_p_kernel(tc, x_words, x_scales, w1, w2, w3, score, o
         nc.sync.dma_start(kept_sb[:], kept)
         score_sb = sb.tile([P, S], F32, name="score_sb")
         nc.sync.dma_start(score_sb[:], score)
-        w2_raw = sb.tile([P, PACK, N], F32, name="w2_raw")
-        nc.sync.dma_start(w2_raw[:], w2.rearrange("(p j) c -> p j c", j=PACK))
         w3_raw = sb.tile([P, PACK, N], F32, name="w3_raw")
         nc.sync.dma_start(w3_raw[:], w3.rearrange("(p j) c -> p j c", j=PACK))
+        w2_raw = sb.tile([P, PACK, N], F32, name="w2_raw")
+        nc.sync.dma_start(w2_raw[:], w2.rearrange("(p j) c -> p j c", j=PACK))
         nc.vector.memset(up[:], 0.0)
 
         x_codes = sb.tile([P, S], U32, name="x_codes", align_bytes=64)
@@ -108,39 +108,39 @@ def tile_picked_ygunet_relu_p_kernel(tc, x_words, x_scales, w1, w2, w3, score, o
         score_kept = sb.tile([P, V], F32, name="score_kept")
         nc.vector.tensor_copy(score_kept[:], score_sb[:].indirect(kept_sb[:]))
 
-        w2_bf = sb.tile([P, N * PACK], BF16, name="w2_bf", tag="w1_bf1", align_bytes=64)
-        nc.vector.tensor_copy(*interleave_views(w2_bf[:], w2_raw[:]))
-        w2_q = quantize("w2", w2_bf[:], N)
+        w3_bf = sb.tile([P, N * PACK], BF16, name="w3_bf", tag="w1_bf1", align_bytes=64)
+        nc.vector.tensor_copy(*interleave_views(w3_bf[:], w3_raw[:]))
+        w3_q = quantize("w3", w3_bf[:], N)
+        y_acc = ps.tile([P, S], F32, name="y_acc", tag="bank2")
+        product(y_acc[:], w3_q, (x_codes[:], x_plane[:]))
 
-        w3_bf = sb.tile([P, N * PACK], BF16, name="w3_bf", tag="w1_3_plane", align_bytes=64)
-        nc.scalar.activation(*interleave_views(w3_bf[:], w3_raw[:]), COPY)
+        w2_bf = sb.tile([P, N * PACK], BF16, name="w2_bf", tag="w1_3_plane", align_bytes=64)
+        nc.scalar.activation(*interleave_views(w2_bf[:], w2_raw[:]), COPY)
+        w2_q = quantize("w2", w2_bf[:], N)
 
         z = sb.tile([P, PACK, V], F32, name="z")
         last = PACK - 1
         for t in range(last):
             nc.vector.tensor_tensor(z[:, t, :], h[t][:].indirect(kept_sb[:]), score_kept[:], MULT)
-        for lo, hi in ((0, PART), (PART, 2 * PART), (2 * PART, V)):
+        for lo, hi in ((PART, 2 * PART), (0, PART), (2 * PART, V)):
             nc.vector.tensor_tensor(z[:, last, lo:hi], h[last][:].indirect(list_columns(lo, hi)), score_kept[:, lo:hi], MULT)
 
-        rr = sb.tile([P, V], F32, name="rr")
+        rr_first = sb.tile([P, PART], F32, name="rr_first")
+        rr_rest = sb.tile([P, V - PART], F32, name="rr_rest")
         for a in range(PARTS):
-            zb = sb.tile([P, PART * PACK], BF16, name=f"z_bf{a}", tag=f"z_bf{a % 3}", align_bytes=64)
+            zb = sb.tile([P, PART * PACK], BF16, name=f"z_bf{a}", tag=f"z_bf{a}", align_bytes=64)
             dst, src = interleave_views(zb[:], z[:, :, a * PART : (a + 1) * PART])
-            if a in (3,):
+            if a in (0,):
                 nc.vector.tensor_copy(dst, src)
             else:
                 nc.scalar.activation(dst, src, COPY)
             z_q = quantize(f"z{a}", zb[:], PART)
-            acc = ps.tile([P, PART], F32, name=f"rr_acc{a}", tag=f"bank{a + 2}")
+            acc = ps.tile([P, PART], F32, name=f"rr_acc{a}", tag=f"bank{a + 3}")
             product(acc[:], w2_q, z_q)
-            nc.scalar.activation(rr[:, a * PART : (a + 1) * PART], acc[:], RELU)
+            nc.scalar.activation(rr_first[:] if a == 0 else rr_rest[:, (a - 1) * PART : a * PART], acc[:], RELU)
 
-        w3_q = quantize("w3", w3_bf[:], N)
-        y_acc = ps.tile([P, S], F32, name="y_acc", tag="bank4")
-        product(y_acc[:], w3_q, (x_codes[:], x_plane[:]))
-
-        for lo, hi in ((0, PART), (PART, V)):
-            nc.vector.tensor_copy(up[:].indirect(list_columns(lo, hi)), rr[:, lo:hi])
+        nc.vector.tensor_copy(up[:].indirect(list_columns(0, PART)), rr_first[:])
+        nc.vector.tensor_copy(up[:].indirect(list_columns(PART, V)), rr_rest[:])
 
         for c in range(2):
             cols = slice(c * HALF_S, (c + 1) * HALF_S)

@@ -21,11 +21,13 @@ P = 128
 PACK = 4
 QUADRANT = 32
 PER_COLUMN = 16
+BANKS = 8
 HALF_S = S // 2
+QUARTER_S = S // 4
 HALF_V = V // 2
 PARTS = 4
 PART = V // PARTS
-VECTOR_PARTS = 2
+Y_BANK = 2
 
 
 def tile_picked_ygunet_relu_p_kernel(tc, x_words, x_scales, w1, w2, w3, score, offs, kept, out):
@@ -96,10 +98,10 @@ def tile_picked_ygunet_relu_p_kernel(tc, x_words, x_scales, w1, w2, w3, score, o
         for t in range(PACK):
             w1_q = quantize(f"w1_{t}", w1_bf[t // 2][:, t % 2, :], P)
             h_t = sb.tile([P, S], F32, name=f"h{t}")
-            width = HALF_S // 2 if t == 0 else HALF_S
+            width = QUARTER_S if t == 0 else HALF_S
             for lo in range(0, S, width):
                 cols = slice(lo, lo + width)
-                acc = ps.tile([P, width], F32, name=f"h_acc{t}_{lo}", tag=f"bank{pieces % 8}")
+                acc = ps.tile([P, width], F32, name=f"h_acc{t}_{lo}", tag=f"bank{pieces % BANKS}")
                 pieces = pieces + 1
                 product(acc[:], w1_q, (x_codes[:, cols], x_plane[:, cols]))
                 nc.scalar.activation(h_t[:, cols], acc[:], RELU)
@@ -111,7 +113,7 @@ def tile_picked_ygunet_relu_p_kernel(tc, x_words, x_scales, w1, w2, w3, score, o
         w3_bf = sb.tile([P, N * PACK], BF16, name="w3_bf", tag="w1_bf1", align_bytes=64)
         nc.vector.tensor_copy(*interleave_views(w3_bf[:], w3_raw[:]))
         w3_q = quantize("w3", w3_bf[:], N)
-        y_acc = ps.tile([P, S], F32, name="y_acc", tag="bank2")
+        y_acc = ps.tile([P, S], F32, name="y_acc", tag=f"bank{Y_BANK}")
         product(y_acc[:], w3_q, (x_codes[:], x_plane[:]))
 
         w2_bf = sb.tile([P, N * PACK], BF16, name="w2_bf", tag="w1_3_plane", align_bytes=64)
@@ -122,22 +124,24 @@ def tile_picked_ygunet_relu_p_kernel(tc, x_words, x_scales, w1, w2, w3, score, o
         last = PACK - 1
         for t in range(last):
             nc.vector.tensor_tensor(z[:, t, :], h[t][:].indirect(kept_sb[:]), score_kept[:], MULT)
-        for lo, hi in ((PART, 2 * PART), (0, PART), (2 * PART, V)):
-            nc.vector.tensor_tensor(z[:, last, lo:hi], h[last][:].indirect(list_columns(lo, hi)), score_kept[:, lo:hi], MULT)
+        for lo in range(0, V, HALF_V):
+            nc.vector.tensor_tensor(z[:, last, lo : lo + HALF_V], h[last][:].indirect(list_columns(lo, lo + HALF_V)),
+                                    score_kept[:, lo : lo + HALF_V], MULT)
 
         rr_first = sb.tile([P, PART], F32, name="rr_first")
         rr_rest = sb.tile([P, V - PART], F32, name="rr_rest")
         for a in range(PARTS):
-            zb = sb.tile([P, PART * PACK], BF16, name=f"z_bf{a}", tag=f"z_bf{a}", align_bytes=64)
+            zb = sb.tile([P, PART * PACK], BF16, name=f"z_bf{a}", align_bytes=64)
             dst, src = interleave_views(zb[:], z[:, :, a * PART : (a + 1) * PART])
-            if a in (0,):
+            if a == 0:
                 nc.vector.tensor_copy(dst, src)
             else:
                 nc.scalar.activation(dst, src, COPY)
             z_q = quantize(f"z{a}", zb[:], PART)
-            acc = ps.tile([P, PART], F32, name=f"rr_acc{a}", tag=f"bank{a + 3}")
+            acc = ps.tile([P, PART], F32, name=f"rr_acc{a}", tag=f"bank{Y_BANK + 1 + a}")
             product(acc[:], w2_q, z_q)
-            nc.scalar.activation(rr_first[:] if a == 0 else rr_rest[:, (a - 1) * PART : a * PART], acc[:], RELU)
+            rr_part = rr_first[:] if a == 0 else rr_rest[:, (a - 1) * PART : a * PART]
+            nc.scalar.activation(rr_part, acc[:], RELU)
 
         nc.vector.tensor_copy(up[:].indirect(list_columns(0, PART)), rr_first[:])
         nc.vector.tensor_copy(up[:].indirect(list_columns(PART, V)), rr_rest[:])

@@ -61,9 +61,8 @@ def tile_picked_ygunet_relu_p_kernel(tc, x_words, x_scales, w1, w2, w3, score, o
         nc.vector.memset(scales_all[:].bitcast(I32), 0)
         nc.sync.dma_start(words_all[:], x_words[0].rearrange("p c r -> p (c r)").bitcast(I32))
         nc.sync.dma_start(offs_sb[:], offs)
-        for q in range(P // QUADRANT):
-            nc.sync.dma_start(scales_all[QUADRANT * q : QUADRANT * q + 4, :].bitcast(I32),
-                              x_scales[0, 4 * q : 4 * q + 4, :].bitcast(I32))
+        for r in range(PACK):
+            nc.sync.dma_start(scales_all[r : P : QUADRANT, :].bitcast(I32), x_scales[0, r : 16 : PACK, :].bitcast(I32))
         w1_rows = w1.rearrange("(p j) c -> p j c", j=PACK)
         w1_raw = []
         for half in range(2):

@@ -57,6 +57,7 @@ def tile_picked_ygunet_relu_p_kernel(tc, x_words, x_scales, w1, w2, w3, score, o
         words_all = sb.tile([P, T], I32, name="words_all")
         scales_all = sb.tile([P, T], U8, name="scales_all")
         up = sb.tile([P, S], F32, name="up")
+        up_first = sb.tile([P, S], F32, name="up_first")
 
         nc.vector.memset(scales_all[:].bitcast(I32), 0)
         nc.sync.dma_start(words_all[:], x_words[0].rearrange("p c r -> p (c r)").bitcast(I32))
@@ -77,6 +78,7 @@ def tile_picked_ygunet_relu_p_kernel(tc, x_words, x_scales, w1, w2, w3, score, o
         w2_raw = sb.tile([P, PACK, N], F32, name="w2_raw")
         nc.sync.dma_start(w2_raw[:], w2.rearrange("(p j) c -> p j c", j=PACK))
         nc.vector.memset(up[:], 0.0)
+        nc.vector.memset(up_first[:], 0.0)
 
         x_codes = sb.tile([P, S], U32, name="x_codes", align_bytes=64)
         x_plane = sb.tile([P, S], U8, name="x_plane", align_bytes=64)
@@ -118,6 +120,8 @@ def tile_picked_ygunet_relu_p_kernel(tc, x_words, x_scales, w1, w2, w3, score, o
         w2_bf = sb.tile([P, N * PACK], BF16, name="w2_bf", tag="w1_3_plane", align_bytes=64)
         nc.scalar.activation(*interleave_views(w2_bf[:], w2_raw[:]), COPY)
         w2_q = quantize("w2", w2_bf[:], N)
+        y_sb = sb.tile([P, HALF_S], F32, name="y_sb")
+        nc.scalar.activation(y_sb[:], y_acc[:, 0:HALF_S], COPY)
 
         z = sb.tile([P, PACK, V], F32, name="z")
         last = PACK - 1
@@ -142,11 +146,17 @@ def tile_picked_ygunet_relu_p_kernel(tc, x_words, x_scales, w1, w2, w3, score, o
             rr_part = rr_first[:] if a == 0 else rr_rest[:, (a - 1) * PART : a * PART]
             nc.scalar.activation(rr_part, acc[:], RELU)
 
+        y_late = sb.tile([P, HALF_S], F32, name="y_late", tag=f"z{PARTS - 1}_codes", align_bytes=64)
+        nc.scalar.activation(y_late[:], y_acc[:, HALF_S:S], COPY)
         nc.vector.tensor_copy(up[:].indirect(list_columns(0, PART)), rr_first[:])
-        nc.vector.tensor_copy(up[:].indirect(list_columns(PART, V)), rr_rest[:])
+        nc.vector.tensor_copy(up_first[:].indirect(list_columns(PART, 2 * PART)), rr_rest[:, 0:PART])
+        nc.vector.tensor_copy(up[:].indirect(list_columns(2 * PART, V)), rr_rest[:, PART : V - PART])
 
+        part = [sb.tile([P, HALF_S], F32, name="part0"), sb.tile([P, HALF_S], F32, name="part1")]
+        nc.gpsimd.tensor_tensor(part[0][:], y_sb[:], up_first[:, 0:HALF_S], ADD)
+        nc.vector.tensor_tensor(part[1][:], y_late[:], up_first[:, HALF_S:S], ADD)
         for c in range(2):
             cols = slice(c * HALF_S, (c + 1) * HALF_S)
             res = sb.tile([P, HALF_S], F32, name=f"res{c}")
-            nc.vector.tensor_tensor(res[:], y_acc[:, cols], up[:, cols], ADD)
+            nc.vector.tensor_tensor(res[:], part[c][:], up[:, cols], ADD)
             nc.sync.dma_start(out[:, cols], res[:])

@@ -114,14 +114,14 @@ def tile_picked_ygunet_relu_p_kernel(tc, x_words, x_scales, w1, w2, w3, score, o
         w3_bf = sb.tile([P, N * PACK], BF16, name="w3_bf", tag="w1_bf1", align_bytes=64)
         nc.vector.tensor_copy(*interleave_views(w3_bf[:], w3_raw[:]))
         w3_q = quantize("w3", w3_bf[:], N)
-        y_acc = ps.tile([P, S], F32, name="y_acc", tag=f"bank{Y_BANK}")
-        product(y_acc[:], w3_q, (x_codes[:], x_plane[:]))
+        y_acc = ps.tile([P, HALF_S], F32, name="y_acc", tag=f"bank{Y_BANK}")
+        product(y_acc[:], w3_q, (x_codes[:, 0:HALF_S], x_plane[:, 0:HALF_S]))
 
         w2_bf = sb.tile([P, N * PACK], BF16, name="w2_bf", tag="w1_3_plane", align_bytes=64)
         nc.scalar.activation(*interleave_views(w2_bf[:], w2_raw[:]), COPY)
         w2_q = quantize("w2", w2_bf[:], N)
         y_sb = sb.tile([P, HALF_S], F32, name="y_sb")
-        nc.scalar.activation(y_sb[:], y_acc[:, 0:HALF_S], COPY)
+        nc.scalar.activation(y_sb[:], y_acc[:], COPY)
 
         z = sb.tile([P, PACK, V], F32, name="z")
         last = PACK - 1
@@ -146,8 +146,8 @@ def tile_picked_ygunet_relu_p_kernel(tc, x_words, x_scales, w1, w2, w3, score, o
             rr_part = rr_first[:] if a == 0 else rr_rest[:, (a - 1) * PART : a * PART]
             nc.scalar.activation(rr_part, acc[:], RELU)
 
-        y_late = sb.tile([P, HALF_S], F32, name="y_late", tag=f"z{PARTS - 1}_codes", align_bytes=64)
-        nc.scalar.activation(y_late[:], y_acc[:, HALF_S:S], COPY)
+        y_late = ps.tile([P, HALF_S], F32, name="y_late", tag=f"bank{Y_BANK + PARTS}")
+        product(y_late[:], w3_q, (x_codes[:, HALF_S:S], x_plane[:, HALF_S:S]))
         nc.vector.tensor_copy(up[:].indirect(list_columns(0, PART)), rr_first[:])
         nc.vector.tensor_copy(up_first[:].indirect(list_columns(PART, 2 * PART)), rr_rest[:, 0:PART])
         nc.vector.tensor_copy(up[:].indirect(list_columns(2 * PART, V)), rr_rest[:, PART : V - PART])

@@ -24,6 +24,7 @@ PER_COLUMN = 16
 BANKS = 8
 HALF_S = S // 2
 QUARTER_S = S // 4
+Y_SPLIT = 192
 HALF_V = V // 2
 PARTS = 4
 PART = V // PARTS
@@ -114,13 +115,14 @@ def tile_picked_ygunet_relu_p_kernel(tc, x_words, x_scales, w1, w2, w3, score, o
         w3_bf = sb.tile([P, N * PACK], BF16, name="w3_bf", tag="w1_bf1", align_bytes=64)
         nc.vector.tensor_copy(*interleave_views(w3_bf[:], w3_raw[:]))
         w3_q = quantize("w3", w3_bf[:], N)
-        y_acc = ps.tile([P, HALF_S], F32, name="y_acc", tag=f"bank{Y_BANK}")
-        product(y_acc[:], w3_q, (x_codes[:, 0:HALF_S], x_plane[:, 0:HALF_S]))
+        y_acc = ps.tile([P, Y_SPLIT], F32, name="y_acc", tag=f"bank{Y_BANK}")
+        for lo, hi in ((0, QUARTER_S), (QUARTER_S, Y_SPLIT)):
+            product(y_acc[:, lo:hi], w3_q, (x_codes[:, lo:hi], x_plane[:, lo:hi]))
 
         w2_bf = sb.tile([P, N * PACK], BF16, name="w2_bf", tag="w1_3_plane", align_bytes=64)
         nc.scalar.activation(*interleave_views(w2_bf[:], w2_raw[:]), COPY)
         w2_q = quantize("w2", w2_bf[:], N)
-        y_sb = sb.tile([P, HALF_S], F32, name="y_sb")
+        y_sb = sb.tile([P, Y_SPLIT], F32, name="y_sb")
         nc.scalar.activation(y_sb[:], y_acc[:], COPY)
 
         z = sb.tile([P, PACK, V], F32, name="z")
@@ -146,17 +148,18 @@ def tile_picked_ygunet_relu_p_kernel(tc, x_words, x_scales, w1, w2, w3, score, o
             rr_part = rr_first[:] if a == 0 else rr_rest[:, (a - 1) * PART : a * PART]
             nc.scalar.activation(rr_part, acc[:], RELU)
 
-        y_late = ps.tile([P, HALF_S], F32, name="y_late", tag=f"bank{Y_BANK + PARTS}")
-        product(y_late[:], w3_q, (x_codes[:, HALF_S:S], x_plane[:, HALF_S:S]))
+        y_late = ps.tile([P, S - Y_SPLIT], F32, name="y_late", tag=f"bank{Y_BANK + PARTS - 1}")
+        for lo, hi in ((Y_SPLIT, HALF_S), (HALF_S, S)):
+            product(y_late[:, lo - Y_SPLIT : hi - Y_SPLIT], w3_q, (x_codes[:, lo:hi], x_plane[:, lo:hi]))
         nc.vector.tensor_copy(up[:].indirect(list_columns(0, PART)), rr_first[:])
         nc.vector.tensor_copy(up_first[:].indirect(list_columns(PART, 2 * PART)), rr_rest[:, 0:PART])
         nc.vector.tensor_copy(up[:].indirect(list_columns(2 * PART, V)), rr_rest[:, PART : V - PART])
 
-        part = [sb.tile([P, HALF_S], F32, name="part0"), sb.tile([P, HALF_S], F32, name="part1")]
-        nc.gpsimd.tensor_tensor(part[0][:], y_sb[:], up_first[:, 0:HALF_S], ADD)
-        nc.vector.tensor_tensor(part[1][:], y_late[:], up_first[:, HALF_S:S], ADD)
-        for c in range(2):
-            cols = slice(c * HALF_S, (c + 1) * HALF_S)
-            res = sb.tile([P, HALF_S], F32, name=f"res{c}")
+        pieces = (slice(0, Y_SPLIT), slice(Y_SPLIT, S))
+        part = [sb.tile([P, cols.stop - cols.start], F32, name=f"part{c}") for c, cols in enumerate(pieces)]
+        nc.gpsimd.tensor_tensor(part[0][:], y_sb[:], up_first[:, pieces[0]], ADD)
+        nc.vector.tensor_tensor(part[1][:], y_late[:], up_first[:, pieces[1]], ADD)
+        for c, cols in enumerate(pieces):
+            res = sb.tile([P, cols.stop - cols.start], F32, name=f"res{c}")
             nc.vector.tensor_tensor(res[:], part[c][:], up[:, cols], ADD)
             nc.sync.dma_start(out[:, cols], res[:])

@@ -37,8 +37,8 @@ def tile_picked_ygunet_relu_p_kernel(tc, x_words, x_scales, w1, w2, w3, score, o
         sb = ctx.enter_context(tc.tile_pool(name="sb", bufs=1))
         ps = ctx.enter_context(tc.psum_pool(name="ps", bufs=1))
 
-        def quantize(name, grouped, width):
-            codes = sb.tile([P, width], U32, name=name + "_codes", tag=name + "_codes", align_bytes=64)
+        def quantize(name, grouped, width, tag=None):
+            codes = sb.tile([P, width], U32, name=name + "_codes", tag=tag or name + "_codes", align_bytes=64)
             scales = sb.tile([P, width], U8, name=name + "_plane", tag=name + "_plane", align_bytes=64)
             nc.vector.quantize_mx(out=codes[:].bitcast(FP8X4), scales=scales[:], in_=grouped)
             return codes[:], scales[:]
@@ -68,7 +68,7 @@ def tile_picked_ygunet_relu_p_kernel(tc, x_words, x_scales, w1, w2, w3, score, o
         w1_rows = w1.rearrange("(p j) c -> p j c", j=PACK)
         w1_raw = []
         for half in range(2):
-            raw = sb.tile([P, 2, H], F32, name=f"w1_raw{half}")
+            raw = sb.tile([P, 2, H], F32, name=f"w1_raw{half}", tag=f"w1_raw{half}", align_bytes=64)
             nc.sync.dma_start(raw[:], w1_rows[:, 2 * half : 2 * half + 2, :])
             w1_raw.append(raw)
         nc.sync.dma_start(kept_sb[:], kept)
@@ -112,7 +112,7 @@ def tile_picked_ygunet_relu_p_kernel(tc, x_words, x_scales, w1, w2, w3, score, o
         score_kept = sb.tile([P, V], F32, name="score_kept")
         nc.vector.tensor_copy(score_kept[:], score_sb[:].indirect(kept_sb[:]))
 
-        w3_bf = sb.tile([P, N * PACK], BF16, name="w3_bf", tag="w1_bf1", align_bytes=64)
+        w3_bf = sb.tile([P, N * PACK], BF16, name="w3_bf", tag="w1_raw1", align_bytes=64)
         nc.vector.tensor_copy(*interleave_views(w3_bf[:], w3_raw[:]))
         w3_q = quantize("w3", w3_bf[:], N)
         y_acc = ps.tile([P, Y_SPLIT], F32, name="y_acc", tag=f"bank{Y_BANK}")
@@ -136,13 +136,13 @@ def tile_picked_ygunet_relu_p_kernel(tc, x_words, x_scales, w1, w2, w3, score, o
         rr_first = sb.tile([P, PART], F32, name="rr_first")
         rr_rest = sb.tile([P, V - PART], F32, name="rr_rest")
         for a in range(PARTS):
-            zb = sb.tile([P, PART * PACK], BF16, name=f"z_bf{a}", align_bytes=64)
+            zb = sb.tile([P, PART * PACK], BF16, name=f"z_bf{a}", tag=f"z_bf{a}", align_bytes=64)
             dst, src = interleave_views(zb[:], z[:, :, a * PART : (a + 1) * PART])
-            if a == 0:
+            if a == 1:
                 nc.vector.tensor_copy(dst, src)
             else:
                 nc.scalar.activation(dst, src, COPY)
-            z_q = quantize(f"z{a}", zb[:], PART)
+            z_q = quantize(f"z{a}", zb[:], PART, tag="z_bf0" if a == 1 else None)
             acc = ps.tile([P, PART], F32, name=f"rr_acc{a}", tag=f"bank{Y_BANK + 1 + a}")
             product(acc[:], w2_q, z_q)
             rr_part = rr_first[:] if a == 0 else rr_rest[:, (a - 1) * PART : a * PART]

@@ -129,20 +129,16 @@ def tile_picked_ygunet_relu_p_kernel(tc, x_words, x_scales, w1, w2, w3, score, o
         last = PACK - 1
         for t in range(last):
             nc.vector.tensor_tensor(z[:, t, :], h[t][:].indirect(kept_sb[:]), score_kept[:], MULT)
-        for lo in range(0, V, HALF_V):
-            nc.vector.tensor_tensor(z[:, last, lo : lo + HALF_V], h[last][:].indirect(list_columns(lo, lo + HALF_V)),
-                                    score_kept[:, lo : lo + HALF_V], MULT)
+        for lo, hi in ((0, PART), (PART, HALF_V), (HALF_V, V)):
+            nc.vector.tensor_tensor(z[:, last, lo:hi], h[last][:].indirect(list_columns(lo, hi)), score_kept[:, lo:hi], MULT)
 
         rr_first = sb.tile([P, PART], F32, name="rr_first")
         rr_rest = sb.tile([P, V - PART], F32, name="rr_rest")
         for a in range(PARTS):
             zb = sb.tile([P, PART * PACK], BF16, name=f"z_bf{a}", tag=f"z_bf{a}", align_bytes=64)
             dst, src = interleave_views(zb[:], z[:, :, a * PART : (a + 1) * PART])
-            if a == 1:
-                nc.vector.tensor_copy(dst, src)
-            else:
-                nc.scalar.activation(dst, src, COPY)
-            z_q = quantize(f"z{a}", zb[:], PART, tag="z_bf0" if a == 1 else None)
+            nc.scalar.activation(dst, src, COPY)
+            z_q = quantize(f"z{a}", zb[:], PART)
             acc = ps.tile([P, PART], F32, name=f"rr_acc{a}", tag=f"bank{Y_BANK + 1 + a}")
             product(acc[:], w2_q, z_q)
             rr_part = rr_first[:] if a == 0 else rr_rest[:, (a - 1) * PART : a * PART]

@@ -122,8 +122,6 @@ def tile_picked_ygunet_relu_p_kernel(tc, x_words, x_scales, w1, w2, w3, score, o
         w2_bf = sb.tile([P, N * PACK], BF16, name="w2_bf", tag="w1_3_plane", align_bytes=64)
         nc.scalar.activation(*interleave_views(w2_bf[:], w2_raw[:]), COPY)
         w2_q = quantize("w2", w2_bf[:], N)
-        y_sb = sb.tile([P, Y_SPLIT], F32, name="y_sb")
-        nc.scalar.activation(y_sb[:], y_acc[:], COPY)
 
         z = sb.tile([P, PACK, V], F32, name="z")
         last = PACK - 1
@@ -135,14 +133,20 @@ def tile_picked_ygunet_relu_p_kernel(tc, x_words, x_scales, w1, w2, w3, score, o
         rr_first = sb.tile([P, PART], F32, name="rr_first")
         rr_rest = sb.tile([P, V - PART], F32, name="rr_rest")
         for a in range(PARTS):
-            zb = sb.tile([P, PART * PACK], BF16, name=f"z_bf{a}", tag=f"z_bf{a}", align_bytes=64)
+            zb = sb.tile([P, PART * PACK], BF16, name=f"z_bf{a}", tag="z_bf0" if a == 2 else f"z_bf{a}", align_bytes=64)
             dst, src = interleave_views(zb[:], z[:, :, a * PART : (a + 1) * PART])
-            nc.scalar.activation(dst, src, COPY)
+            if a == 2:
+                nc.vector.tensor_copy(dst, src)
+            else:
+                nc.scalar.activation(dst, src, COPY)
             z_q = quantize(f"z{a}", zb[:], PART)
             acc = ps.tile([P, PART], F32, name=f"rr_acc{a}", tag=f"bank{Y_BANK + 1 + a}")
             product(acc[:], w2_q, z_q)
             rr_part = rr_first[:] if a == 0 else rr_rest[:, (a - 1) * PART : a * PART]
             nc.scalar.activation(rr_part, acc[:], RELU)
+
+        y_sb = sb.tile([P, Y_SPLIT], F32, name="y_sb", tag="z2_codes", align_bytes=64)
+        nc.scalar.activation(y_sb[:], y_acc[:], COPY)
 
         y_late = ps.tile([P, S - Y_SPLIT], F32, name="y_late", tag=f"bank{Y_BANK + PARTS - 1}")
         for lo, hi in ((Y_SPLIT, HALF_S), (HALF_S, S)):

from contextlib import ExitStack

import concourse.mybir as mybir

K, T, S, H, N, V = 512, 1024, 512, 512, 128, 256
FLOPS = 2 * K * H * S + 2 * H * N * V + 2 * K * N * S

F32 = mybir.dt.float32
BF16 = mybir.dt.bfloat16
I32 = mybir.dt.int32
U32 = mybir.dt.uint32
U16 = mybir.dt.uint16
U8 = mybir.dt.uint8
FP8X4 = mybir.dt.float8_e4m3fn_x4
RELU = mybir.ActivationFunctionType.Relu
COPY = mybir.ActivationFunctionType.Copy
MULT = mybir.AluOpType.mult
ADD = mybir.AluOpType.add

P = 128
PACK = 4
QUADRANT = 32
PER_COLUMN = 16
BANKS = 8
HALF_S = S // 2
QUARTER_S = S // 4
Y_SPLIT = 192
HALF_V = V // 2
PARTS = 4
PART = V // PARTS
Y_BANK = 2


def tile_picked_ygunet_relu_p_kernel(tc, x_words, x_scales, w1, w2, w3, score, offs, kept, out):
    nc = tc.nc
    with ExitStack() as ctx:
        sb = ctx.enter_context(tc.tile_pool(name="sb", bufs=1))
        ps = ctx.enter_context(tc.psum_pool(name="ps", bufs=1))

        def quantize(name, grouped, width, tag=None):
            codes = sb.tile([P, width], U32, name=name + "_codes", tag=tag or name + "_codes", align_bytes=64)
            scales = sb.tile([P, width], U8, name=name + "_plane", tag=name + "_plane", align_bytes=64)
            nc.vector.quantize_mx(out=codes[:].bitcast(FP8X4), scales=scales[:], in_=grouped)
            return codes[:], scales[:]

        def product(acc, lhs, rhs):
            nc.tensor.matmul_mx(out=acc, lhsT=lhs[0].bitcast(FP8X4), lhsT_scale=lhs[1],
                                rhs=rhs[0].bitcast(FP8X4), rhs_scale=rhs[1], start=True, stop=True)

        def interleave_views(dst, src):
            return (dst.rearrange("p (c i j) -> p c j i", i=4, j=PACK), src.rearrange("p j (c i) -> p c j i", i=4))

        def list_columns(lo, hi):
            return kept_sb[:, lo // PER_COLUMN : hi // PER_COLUMN]

        offs_sb = sb.tile([P, S // PER_COLUMN], U16, name="offs_sb")
        kept_sb = sb.tile([P, V // PER_COLUMN], U16, name="kept_sb")
        words_all = sb.tile([P, T], I32, name="words_all")
        scales_all = sb.tile([P, T], U8, name="scales_all")
        up = sb.tile([P, S], F32, name="up")
        up_first = sb.tile([P, S], F32, name="up_first")

        nc.vector.memset(scales_all[:].bitcast(I32), 0)
        nc.sync.dma_start(words_all[:], x_words[0].rearrange("p c r -> p (c r)").bitcast(I32))
        nc.sync.dma_start(offs_sb[:], offs)
        for r in range(PACK):
            nc.sync.dma_start(scales_all[r : P : QUADRANT, :].bitcast(I32), x_scales[0, r : 16 : PACK, :].bitcast(I32))
        w1_rows = w1.rearrange("(p j) c -> p j c", j=PACK)
        w1_raw = []
        for half in range(2):
            raw = sb.tile([P, 2, H], F32, name=f"w1_raw{half}", tag=f"w1_raw{half}", align_bytes=64)
            nc.sync.dma_start(raw[:], w1_rows[:, 2 * half : 2 * half + 2, :])
            w1_raw.append(raw)
        nc.sync.dma_start(kept_sb[:], kept)
        score_sb = sb.tile([P, S], F32, name="score_sb")
        nc.sync.dma_start(score_sb[:], score)
        w3_raw = sb.tile([P, PACK, N], F32, name="w3_raw")
        nc.sync.dma_start(w3_raw[:], w3.rearrange("(p j) c -> p j c", j=PACK))
        w2_raw = sb.tile([P, PACK, N], F32, name="w2_raw")
        nc.sync.dma_start(w2_raw[:], w2.rearrange("(p j) c -> p j c", j=PACK))
        nc.vector.memset(up[:], 0.0)
        nc.vector.memset(up_first[:], 0.0)

        x_codes = sb.tile([P, S], U32, name="x_codes", align_bytes=64)
        x_plane = sb.tile([P, S], U8, name="x_plane", align_bytes=64)
        nc.vector.tensor_copy(x_codes[:], words_all[:].bitcast(U32).indirect(offs_sb[:]))
        nc.vector.tensor_copy(x_plane[:], scales_all[:].indirect(offs_sb[:]))

        w1_bf = [sb.tile([P, 2, P * PACK], BF16, name=f"w1_bf{u}", tag=f"w1_bf{u}", align_bytes=64) for u in range(2)]
        w1_dst = [bf[:].rearrange("p t (m j) -> p m t j", j=PACK) for bf in w1_bf]
        w1_src = [raw[:].rearrange("p j (m t) -> p m t j", t=PACK) for raw in w1_raw]
        for u in range(2):
            nc.scalar.activation(w1_dst[u][:, :, :, 0:2], w1_src[0][:, :, 2 * u : 2 * u + 2], COPY)
        for t in range(2):
            nc.vector.tensor_copy(w1_dst[0][:, :, t, 2:4], w1_src[1][:, :, t])
        nc.scalar.activation(w1_dst[1][:, :, :, 2:4], w1_src[1][:, :, 2:4], COPY)

        h = []
        pieces = 0
        for t in range(PACK):
            w1_q = quantize(f"w1_{t}", w1_bf[t // 2][:, t % 2, :], P)
            h_t = sb.tile([P, S], F32, name=f"h{t}")
            width = QUARTER_S if t == 0 else HALF_S
            for lo in range(0, S, width):
                cols = slice(lo, lo + width)
                acc = ps.tile([P, width], F32, name=f"h_acc{t}_{lo}", tag=f"bank{pieces % BANKS}")
                pieces = pieces + 1
                product(acc[:], w1_q, (x_codes[:, cols], x_plane[:, cols]))
                nc.scalar.activation(h_t[:, cols], acc[:], RELU)
            h.append(h_t)

        score_kept = sb.tile([P, V], F32, name="score_kept")
        nc.vector.tensor_copy(score_kept[:], score_sb[:].indirect(kept_sb[:]))

        w3_bf = sb.tile([P, N * PACK], BF16, name="w3_bf", tag="w1_raw1", align_bytes=64)
        nc.vector.tensor_copy(*interleave_views(w3_bf[:], w3_raw[:]))
        w3_q = quantize("w3", w3_bf[:], N)
        y_acc = ps.tile([P, Y_SPLIT], F32, name="y_acc", tag=f"bank{Y_BANK}")
        for lo, hi in ((0, QUARTER_S), (QUARTER_S, Y_SPLIT)):
            product(y_acc[:, lo:hi], w3_q, (x_codes[:, lo:hi], x_plane[:, lo:hi]))

        w2_bf = sb.tile([P, N * PACK], BF16, name="w2_bf", tag="w1_3_plane", align_bytes=64)
        nc.scalar.activation(*interleave_views(w2_bf[:], w2_raw[:]), COPY)
        w2_q = quantize("w2", w2_bf[:], N)

        z = sb.tile([P, PACK, V], F32, name="z")
        last = PACK - 1
        for t in range(last):
            nc.vector.tensor_tensor(z[:, t, :], h[t][:].indirect(kept_sb[:]), score_kept[:], MULT)
        for lo, hi in ((0, PART), (PART, HALF_V), (HALF_V, V)):
            nc.vector.tensor_tensor(z[:, last, lo:hi], h[last][:].indirect(list_columns(lo, hi)), score_kept[:, lo:hi], MULT)

        rr_first = sb.tile([P, PART], F32, name="rr_first")
        rr_rest = sb.tile([P, V - PART], F32, name="rr_rest")
        for a in range(PARTS):
            zb = sb.tile([P, PART * PACK], BF16, name=f"z_bf{a}", tag="z_bf0" if a == 2 else f"z_bf{a}", align_bytes=64)
            dst, src = interleave_views(zb[:], z[:, :, a * PART : (a + 1) * PART])
            if a == 2:
                nc.vector.tensor_copy(dst, src)
            else:
                nc.scalar.activation(dst, src, COPY)
            z_q = quantize(f"z{a}", zb[:], PART)
            acc = ps.tile([P, PART], F32, name=f"rr_acc{a}", tag=f"bank{Y_BANK + 1 + a}")
            product(acc[:], w2_q, z_q)
            rr_part = rr_first[:] if a == 0 else rr_rest[:, (a - 1) * PART : a * PART]
            nc.scalar.activation(rr_part, acc[:], RELU)

        y_sb = sb.tile([P, Y_SPLIT], F32, name="y_sb", tag="z2_codes", align_bytes=64)
        nc.scalar.activation(y_sb[:], y_acc[:], COPY)

        y_late = ps.tile([P, S - Y_SPLIT], F32, name="y_late", tag=f"bank{Y_BANK + PARTS - 1}")
        for lo, hi in ((Y_SPLIT, HALF_S), (HALF_S, S)):
            product(y_late[:, lo - Y_SPLIT : hi - Y_SPLIT], w3_q, (x_codes[:, lo:hi], x_plane[:, lo:hi]))
        nc.vector.tensor_copy(up[:].indirect(list_columns(0, PART)), rr_first[:])
        nc.vector.tensor_copy(up_first[:].indirect(list_columns(PART, 2 * PART)), rr_rest[:, 0:PART])
        nc.vector.tensor_copy(up[:].indirect(list_columns(2 * PART, V)), rr_rest[:, PART : V - PART])

        pieces = (slice(0, Y_SPLIT), slice(Y_SPLIT, S))
        part = [sb.tile([P, cols.stop - cols.start], F32, name=f"part{c}") for c, cols in enumerate(pieces)]
        nc.gpsimd.tensor_tensor(part[0][:], y_sb[:], up_first[:, pieces[0]], ADD)
        nc.vector.tensor_tensor(part[1][:], y_late[:], up_first[:, pieces[1]], ADD)
        for c, cols in enumerate(pieces):
            res = sb.tile([P, cols.stop - cols.start], F32, name=f"res{c}")
            nc.vector.tensor_tensor(res[:], part[c][:], up[:, cols], ADD)
            nc.sync.dma_start(out[:, cols], res[:])
